import numpy as np
import ml_dtypes

BF16 = ml_dtypes.bfloat16


def bf(x):
    return np.asarray(x, np.float32).astype(BF16)


def f32(x):
    return np.asarray(x, np.float32)


def f64(x):
    return np.asarray(x).astype(np.float64)


def striped(idx):
    return np.tile(idx.reshape(-1, 16).T, (8, 1))


S, K, M, N, E, Q = 512, 256, 128, 256, 4, 64


def setup_inputs():
    return {"base": bf(np.random.standard_normal((M, S))), "x": bf(np.random.standard_normal((K, N))), "w": bf(np.random.standard_normal((E, K, M)) / np.sqrt(K)), "c": f32(0.2 + 0.8 * np.random.random_sample((1, S))), "offs": striped(np.random.permutation(S)[:N])}


def reference(base, x, w, c, offs):
    idx = offs[:16].T.reshape(-1)
    z = f64(base).copy()
    for e in range(E):
        z[:, idx[e * Q : (e + 1) * Q]] += f64(w)[e].T @ f64(x)[:, e * Q : (e + 1) * Q]
    return z * f64(c)

@@ -1,0 +1,54 @@
+import concourse.mybir as mybir
+from concourse.masks import make_identity
+
+BF16, F32, U16 = mybir.dt.bfloat16, mybir.dt.float32, mybir.dt.uint16
+
+P = 128
+S = 512
+K = 256
+N = 256
+E = 4
+Q = N // E
+KB = K // P
+QC = Q // 16
+
+FLOPS = 2 * K * P * N
+
+
+def tile_scatter_matmul_kernel(tc, base, x, w, c, offs, out):
+    nc = tc.nc
+    with (
+        tc.tile_pool(name="held", bufs=1) as held,
+        tc.psum_pool(name="psum", bufs=1) as psum,
+    ):
+        offsets = held.tile([P, N // 16], U16, name="offsets")
+        nc.sync.dma_start(offsets[:], offs)
+        base_sb = held.tile([P, S], BF16, name="base_sb")
+        nc.scalar.dma_start(base_sb[:], base)
+        x_sb = held.tile([P, KB, N], BF16, name="x_sb")
+        nc.sync.dma_start(x_sb[:], x.rearrange("(kb p) n -> p kb n", p=P))
+        w_sb = held.tile([P, E * KB, P], BF16, name="w_sb")
+        nc.scalar.dma_start(w_sb[:], w.rearrange("e (kb p) m -> p (e kb) m", p=P))
+        c_all = held.tile([P, S], F32, name="c_all")
+        nc.sync.dma_start(c_all[:], c.rearrange("o s -> (o s)").partition_broadcast(P))
+
+        ident = held.tile([P, P], BF16, name="ident")
+        make_identity(nc, ident[:])
+
+        window = psum.tile([P, S], F32, name="window")
+        nc.tensor.matmul(window[:], ident[:], base_sb[:], start=True, stop=False)
+
+        for e in range(E):
+            places = window[:].indirect(offsets[:, e * QC : (e + 1) * QC])
+            for kb in range(KB):
+                nc.tensor.matmul(
+                    places,
+                    w_sb[:, e * KB + kb, :],
+                    x_sb[:, kb, e * Q : (e + 1) * Q],
+                    start=False,
+                    stop=(e == E - 1 and kb == KB - 1),
+                )
+
+        out_sb = held.tile([P, S], F32, name="out_sb")
+        nc.vector.tensor_tensor(out_sb[:], window[:], c_all[:], mybir.AluOpType.mult)
+        nc.sync.dma_start(out, out_sb[:])

@@ -10,7 +10,10 @@ N = 256
 E = 4
 Q = N // E
 KB = K // P
+SB = S // P
 QC = Q // 16
+
+WARM = 4
 
 FLOPS = 2 * K * P * N
 
@@ -23,32 +26,63 @@ def tile_scatter_matmul_kernel(tc, base, x, w, c, offs, out):
     ):
         offsets = held.tile([P, N // 16], U16, name="offsets")
         nc.sync.dma_start(offsets[:], offs)
+        c_col = held.tile([P, SB], F32, name="c_col")
+        nc.scalar.dma_start(c_col[:], c.rearrange("o (a p) -> p (o a)", p=P))
         base_sb = held.tile([P, S], BF16, name="base_sb")
         nc.scalar.dma_start(base_sb[:], base)
         x_sb = held.tile([P, KB, N], BF16, name="x_sb")
-        nc.sync.dma_start(x_sb[:], x.rearrange("(kb p) n -> p kb n", p=P))
-        w_sb = held.tile([P, E * KB, P], BF16, name="w_sb")
-        nc.scalar.dma_start(w_sb[:], w.rearrange("e (kb p) m -> p (e kb) m", p=P))
-        c_all = held.tile([P, S], F32, name="c_all")
-        nc.sync.dma_start(c_all[:], c.rearrange("o s -> (o s)").partition_broadcast(P))
+        nc.sync.dma_start(x_sb[:], x.rearrange("(p kb) n -> p kb n", p=P))
+        w_sb = []
+        for e in range(E):
+            w_e = held.tile([P, KB, P], BF16, name="w_%d" % e)
+            queue = nc.scalar if e % 2 == 0 else nc.sync
+            queue.dma_start(w_e[:], w[e].rearrange("(p kb) m -> p kb m", p=P))
+            w_sb.append(w_e)
 
+        ident_f32 = held.tile([P, P], F32, name="ident_f32")
+        make_identity(nc, ident_f32[:])
         ident = held.tile([P, P], BF16, name="ident")
-        make_identity(nc, ident[:])
+        nc.vector.tensor_copy(ident[:], ident_f32[:])
+
+        zeros = held.tile([P, P], BF16, name="zeros")
+        nc.vector.memset(zeros[:], 0.0)
+        idle_psum = psum.tile([P, SB, P], F32, name="idle_psum")
+        for i in range(WARM):
+            nc.tensor.matmul(
+                idle_psum[:],
+                zeros[:],
+                zeros[:].unsqueeze(1).to_broadcast([P, SB, P]),
+                start=True,
+                stop=True,
+            )
 
         window = psum.tile([P, S], F32, name="window")
         nc.tensor.matmul(window[:], ident[:], base_sb[:], start=True, stop=False)
+
+        c_psum = psum.tile([P, S], F32, name="c_psum")
+        for a in range(SB):
+            nc.tensor.transpose(
+                c_psum[:, a * P : (a + 1) * P],
+                c_col[:, a : a + 1].to_broadcast([P, P]),
+                ident_f32[:],
+            )
+        c_all = held.tile([P, S], F32, name="c_all")
+        nc.vector.tensor_copy(c_all[:], c_psum[:])
 
         for e in range(E):
             places = window[:].indirect(offsets[:, e * QC : (e + 1) * QC])
             for kb in range(KB):
                 nc.tensor.matmul(
                     places,
-                    w_sb[:, e * KB + kb, :],
+                    w_sb[e][:, kb, :],
                     x_sb[:, kb, e * Q : (e + 1) * Q],
                     start=False,
                     stop=(e == E - 1 and kb == KB - 1),
                 )
 
         out_sb = held.tile([P, S], F32, name="out_sb")
-        nc.vector.tensor_tensor(out_sb[:], window[:], c_all[:], mybir.AluOpType.mult)
-        nc.sync.dma_start(out, out_sb[:])
+        for a in range(SB):
+            cols = slice(a * P, (a + 1) * P)
+            nc.vector.tensor_tensor(out_sb[:, cols], window[:, cols], c_all[:, cols], mybir.AluOpType.mult)
+            queue = nc.sync if a % 2 == 0 else nc.scalar
+            queue.dma_start(out[:, cols], out_sb[:, cols])

@@ -26,8 +26,6 @@ def tile_scatter_matmul_kernel(tc, base, x, w, c, offs, out):
     ):
         offsets = held.tile([P, N // 16], U16, name="offsets")
         nc.sync.dma_start(offsets[:], offs)
-        c_col = held.tile([P, SB], F32, name="c_col")
-        nc.scalar.dma_start(c_col[:], c.rearrange("o (a p) -> p (o a)", p=P))
         base_sb = held.tile([P, S], BF16, name="base_sb")
         nc.scalar.dma_start(base_sb[:], base)
         x_sb = held.tile([P, KB, N], BF16, name="x_sb")
@@ -39,10 +37,11 @@ def tile_scatter_matmul_kernel(tc, base, x, w, c, offs, out):
             queue.dma_start(w_e[:], w[e].rearrange("(p kb) m -> p kb m", p=P))
             w_sb.append(w_e)
 
-        ident_f32 = held.tile([P, P], F32, name="ident_f32")
-        make_identity(nc, ident_f32[:])
+        c_all = held.tile([P, S], F32, name="c_all")
+        nc.sync.dma_start(c_all[:], c.rearrange("o s -> (o s)").partition_broadcast(P))
+
         ident = held.tile([P, P], BF16, name="ident")
-        nc.vector.tensor_copy(ident[:], ident_f32[:])
+        make_identity(nc, ident[:])
 
         zeros = held.tile([P, P], BF16, name="zeros")
         nc.vector.memset(zeros[:], 0.0)
@@ -58,16 +57,6 @@ def tile_scatter_matmul_kernel(tc, base, x, w, c, offs, out):
 
         window = psum.tile([P, S], F32, name="window")
         nc.tensor.matmul(window[:], ident[:], base_sb[:], start=True, stop=False)
-
-        c_psum = psum.tile([P, S], F32, name="c_psum")
-        for a in range(SB):
-            nc.tensor.transpose(
-                c_psum[:, a * P : (a + 1) * P],
-                c_col[:, a : a + 1].to_broadcast([P, P]),
-                ident_f32[:],
-            )
-        c_all = held.tile([P, S], F32, name="c_all")
-        nc.vector.tensor_copy(c_all[:], c_psum[:])
 
         for e in range(E):
             places = window[:].indirect(offsets[:, e * QC : (e + 1) * QC])

@@ -26,6 +26,8 @@ def tile_scatter_matmul_kernel(tc, base, x, w, c, offs, out):
     ):
         offsets = held.tile([P, N // 16], U16, name="offsets")
         nc.sync.dma_start(offsets[:], offs)
+        c_col = held.tile([P, SB], F32, name="c_col")
+        nc.scalar.dma_start(c_col[:], c.rearrange("o (p a) -> p (o a)", p=P))
         base_sb = held.tile([P, S], BF16, name="base_sb")
         nc.scalar.dma_start(base_sb[:], base)
         x_sb = held.tile([P, KB, N], BF16, name="x_sb")
@@ -37,11 +39,10 @@ def tile_scatter_matmul_kernel(tc, base, x, w, c, offs, out):
             queue.dma_start(w_e[:], w[e].rearrange("(p kb) m -> p kb m", p=P))
             w_sb.append(w_e)
 
-        c_all = held.tile([P, S], F32, name="c_all")
-        nc.sync.dma_start(c_all[:], c.rearrange("o s -> (o s)").partition_broadcast(P))
-
+        ident_f32 = held.tile([P, P], F32, name="ident_f32")
+        make_identity(nc, ident_f32[:])
         ident = held.tile([P, P], BF16, name="ident")
-        make_identity(nc, ident[:])
+        nc.vector.tensor_copy(ident[:], ident_f32[:])
 
         zeros = held.tile([P, P], BF16, name="zeros")
         nc.vector.memset(zeros[:], 0.0)
@@ -54,6 +55,17 @@ def tile_scatter_matmul_kernel(tc, base, x, w, c, offs, out):
                 start=True,
                 stop=True,
             )
+
+        c_psum = psum.tile([P, SB, P], F32, name="c_psum")
+        for a in range(SB):
+            nc.tensor.transpose(
+                c_psum[:, a, :],
+                c_col[:, a : a + 1].to_broadcast([P, P]),
+                ident_f32[:],
+            )
+        c_all = held.tile([P, P, SB], F32, name="c_all")
+        nc.vector.tensor_copy(c_all[:], c_psum[:].rearrange("m a p -> m p a"))
+        c_row = c_all[:].rearrange("m p a -> m (p a)")
 
         window = psum.tile([P, S], F32, name="window")
         nc.tensor.matmul(window[:], ident[:], base_sb[:], start=True, stop=False)
@@ -72,6 +84,6 @@ def tile_scatter_matmul_kernel(tc, base, x, w, c, offs, out):
         out_sb = held.tile([P, S], F32, name="out_sb")
         for a in range(SB):
             cols = slice(a * P, (a + 1) * P)
-            nc.vector.tensor_tensor(out_sb[:, cols], window[:, cols], c_all[:, cols], mybir.AluOpType.mult)
+            nc.vector.tensor_tensor(out_sb[:, cols], window[:, cols], c_row[:, cols], mybir.AluOpType.mult)
             queue = nc.sync if a % 2 == 0 else nc.scalar
             queue.dma_start(out[:, cols], out_sb[:, cols])

@@ -24,18 +24,18 @@ def tile_scatter_matmul_kernel(tc, base, x, w, c, offs, out):
         tc.tile_pool(name="held", bufs=1) as held,
         tc.psum_pool(name="psum", bufs=1) as psum,
     ):
-        offsets = held.tile([P, N // 16], U16, name="offsets")
-        nc.sync.dma_start(offsets[:], offs)
         c_col = held.tile([P, SB], F32, name="c_col")
-        nc.scalar.dma_start(c_col[:], c.rearrange("o (p a) -> p (o a)", p=P))
+        nc.sync.dma_start(c_col[:], c.rearrange("o (p a) -> p (o a)", p=P))
         base_sb = held.tile([P, S], BF16, name="base_sb")
         nc.scalar.dma_start(base_sb[:], base)
         x_sb = held.tile([P, KB, N], BF16, name="x_sb")
         nc.sync.dma_start(x_sb[:], x.rearrange("(p kb) n -> p kb n", p=P))
+        offsets = held.tile([P, N // 16], U16, name="offsets")
+        nc.sync.dma_start(offsets[:], offs)
         w_sb = []
         for e in range(E):
             w_e = held.tile([P, KB, P], BF16, name="w_%d" % e)
-            queue = nc.scalar if e % 2 == 0 else nc.sync
+            queue = nc.scalar if e < E - 1 else nc.sync
             queue.dma_start(w_e[:], w[e].rearrange("(p kb) m -> p kb m", p=P))
             w_sb.append(w_e)
 

@@ -13,7 +13,7 @@ KB = K // P
 SB = S // P
 QC = Q // 16
 
-WARM = 4
+WARM = 3
 
 FLOPS = 2 * K * P * N
 

import concourse.mybir as mybir
from concourse.masks import make_identity

BF16, F32, U16 = mybir.dt.bfloat16, mybir.dt.float32, mybir.dt.uint16

P = 128
S = 512
K = 256
N = 256
E = 4
Q = N // E
KB = K // P
SB = S // P
QC = Q // 16

WARM = 3

FLOPS = 2 * K * P * N


def tile_scatter_matmul_kernel(tc, base, x, w, c, offs, out):
    nc = tc.nc
    with (
        tc.tile_pool(name="held", bufs=1) as held,
        tc.psum_pool(name="psum", bufs=1) as psum,
    ):
        c_col = held.tile([P, SB], F32, name="c_col")
        nc.sync.dma_start(c_col[:], c.rearrange("o (p a) -> p (o a)", p=P))
        base_sb = held.tile([P, S], BF16, name="base_sb")
        nc.scalar.dma_start(base_sb[:], base)
        x_sb = held.tile([P, KB, N], BF16, name="x_sb")
        nc.sync.dma_start(x_sb[:], x.rearrange("(p kb) n -> p kb n", p=P))
        offsets = held.tile([P, N // 16], U16, name="offsets")
        nc.sync.dma_start(offsets[:], offs)
        w_sb = []
        for e in range(E):
            w_e = held.tile([P, KB, P], BF16, name="w_%d" % e)
            queue = nc.scalar if e < E - 1 else nc.sync
            queue.dma_start(w_e[:], w[e].rearrange("(p kb) m -> p kb m", p=P))
            w_sb.append(w_e)

        ident_f32 = held.tile([P, P], F32, name="ident_f32")
        make_identity(nc, ident_f32[:])
        ident = held.tile([P, P], BF16, name="ident")
        nc.vector.tensor_copy(ident[:], ident_f32[:])

        zeros = held.tile([P, P], BF16, name="zeros")
        nc.vector.memset(zeros[:], 0.0)
        idle_psum = psum.tile([P, SB, P], F32, name="idle_psum")
        for i in range(WARM):
            nc.tensor.matmul(
                idle_psum[:],
                zeros[:],
                zeros[:].unsqueeze(1).to_broadcast([P, SB, P]),
                start=True,
                stop=True,
            )

        c_psum = psum.tile([P, SB, P], F32, name="c_psum")
        for a in range(SB):
            nc.tensor.transpose(
                c_psum[:, a, :],
                c_col[:, a : a + 1].to_broadcast([P, P]),
                ident_f32[:],
            )
        c_all = held.tile([P, P, SB], F32, name="c_all")
        nc.vector.tensor_copy(c_all[:], c_psum[:].rearrange("m a p -> m p a"))
        c_row = c_all[:].rearrange("m p a -> m (p a)")

        window = psum.tile([P, S], F32, name="window")
        nc.tensor.matmul(window[:], ident[:], base_sb[:], start=True, stop=False)

        for e in range(E):
            places = window[:].indirect(offsets[:, e * QC : (e + 1) * QC])
            for kb in range(KB):
                nc.tensor.matmul(
                    places,
                    w_sb[e][:, kb, :],
                    x_sb[:, kb, e * Q : (e + 1) * Q],
                    start=False,
                    stop=(e == E - 1 and kb == KB - 1),
                )

        out_sb = held.tile([P, S], F32, name="out_sb")
        for a in range(SB):
            cols = slice(a * P, (a + 1) * P)
            nc.vector.tensor_tensor(out_sb[:, cols], window[:, cols], c_row[:, cols], mybir.AluOpType.mult)
            queue = nc.sync if a % 2 == 0 else nc.scalar
            queue.dma_start(out[:, cols], out_sb[:, cols])
